import numpy as np
import ml_dtypes


def mxq(x, axis, fmt="e4m3"):
    dtype, down = {"e4m3": (ml_dtypes.float8_e4m3fn, 7), "e5m2": (ml_dtypes.float8_e5m2, 14)}[fmt]
    v = np.moveaxis(np.asarray(x, np.float32).astype(ml_dtypes.bfloat16).astype(np.float64), axis, -1)
    blocks = v.reshape(v.shape[:-1] + (-1, 32))
    amax = np.abs(blocks).max(-1, keepdims=True)
    byte = np.maximum(np.where(amax > 0, np.frexp(amax)[1] - 1 + 127, 0) - down, 1)
    scale = np.exp2(byte - 127.0)
    codes = (blocks / scale).astype(np.float32).astype(dtype).astype(np.float64)
    return np.moveaxis((codes * scale).reshape(v.shape), -1, axis)


WIDE = False


def mx_kscale(k):
    if not WIDE:
        return np.ones(k)
    levels = np.array([10, -10, 5, -5, 0])
    if k % 512:
        return np.exp2(np.random.permutation(np.resize(levels, k // 32))).repeat(32)
    a = np.empty((k // 512, 16))
    for p in range(k // 512):
        a[p, :8] = np.random.permutation(np.resize(levels, 8))
        for g in range(8):
            far = levels[np.abs(levels - a[p, g]) >= 10]
            a[p, g + 8] = far[np.random.randint(len(far))]
    return np.exp2(a.ravel()).repeat(32)


def f64(x):
    return np.asarray(x).astype(np.float64)


def striped(idx):
    return np.tile(idx.reshape(-1, 16).T, (8, 1)).astype(np.uint16)


def unstriped(offs):
    return offs[:16].T.reshape(-1).astype(np.int64)


def striped8(idx):
    return np.concatenate([x.reshape(-1, 16).T for x in idx]).astype(np.uint16)


def runs(offs, k):
    lists = np.stack([offs[16 * r : 16 * r + 16].T.reshape(-1) for r in range(8)]).astype(np.int64)
    return lists[np.arange(k) % 512 // 64]


def pack_weight(w):
    k, n = w.shape
    w = f64(np.asarray(w, np.float32).astype(ml_dtypes.bfloat16)).reshape(k // 32, 32, n)
    amax = np.abs(w).max(1)
    byte = np.clip(np.where(amax > 0, np.frexp(amax)[1] - 1 + 127 - 7, 1), 1, 254)
    scaled = (w * np.exp2(127.0 - byte)[:, None, :]).reshape(k, n).astype(np.float32)
    words = np.ascontiguousarray(scaled.reshape(k // 512, 128, 4, n).transpose(0, 1, 3, 2)).astype(ml_dtypes.float8_e4m3fn).view(np.uint8)
    return words, np.ascontiguousarray(byte.astype(np.uint8).reshape(k // 512, 16, n))


def unpack_weight(words, scales):
    g, p, n, _ = words.shape
    vals = np.ascontiguousarray(words).view(ml_dtypes.float8_e4m3fn).astype(np.float64) * np.repeat(np.exp2(scales.astype(np.float64) - 127.0), 8, axis=1)[..., None]
    return vals.transpose(0, 1, 3, 2).reshape(g * 512, n)


K, T, S, N, G, H, W, U = 512, 1024, 256, 512, 2048, 512, 128, 1024


def setup_inputs():
    n = np.random.standard_normal
    s = mx_kscale(K)[:, None]
    u = mx_kscale(K)
    packed_xT = pack_weight(n((K, T)) * s)
    packed_dT = pack_weight(n((K, G)) / s)
    perm = np.random.permutation(S)
    return {
        "x_words": packed_xT[0],
        "x_scales": packed_xT[1],
        "d_words": packed_dT[0],
        "d_scales": packed_dT[1],
        "gn": (np.random.uniform(0.5, 1.5, (H, 1)) * u[:, None]).astype(np.float32),
        "w1": (n((H, N)) / np.sqrt(H) / u[:, None]).astype(np.float32),
        "offs": striped8(np.random.randint(0, T, (8, S))),
        "ka": striped8(np.random.randint(0, G, (8, H))),
        "kb": striped8(np.random.randint(0, G, (8, H))),
        "n1": striped(perm[:W]),
        "n2": striped(perm[W:]),
        "n3": striped(np.random.permutation(S)),
        "n4": striped(np.random.permutation(U)[:S]),
        "n5": striped(np.random.permutation(S)),
    }


def reference(x_words, x_scales, d_words, d_scales, gn, w1, offs, ka, kb, n1, n2, n3, n4, n5):
    d_ka = unpack_weight(d_words, d_scales)[np.arange(K)[:, None], runs(ka, K)]
    xq = unpack_weight(x_words, x_scales)[np.arange(K)[:, None], runs(offs, K)]
    d_kb = unpack_weight(d_words, d_scales)[np.arange(K)[:, None], runs(kb, K)]
    h = 0.0625 * (d_ka.T @ xq + d_kb.T @ xq)
    pa = h[:, unstriped(n1)]
    pb = h[:, unstriped(n2)]
    rb = np.minimum(pa, pb)
    ra = np.maximum(pa, pb)
    ds = np.zeros((H, S))
    ds[:, unstriped(n1)] = ra
    dt = ds.copy()
    dt[:, unstriped(n2)] = rb
    z = f64(gn) * (dt - dt[:, unstriped(n3)])
    h2 = mxq(f64(w1), 0, "e4m3").T @ mxq(z, 0, "e4m3")
    nw = np.maximum(h2, h2[:, unstriped(n5)])
    out = np.zeros((N, U))
    out[:, unstriped(n4)] = nw
    return out

@@ -1,0 +1,198 @@
+from contextlib import ExitStack
+
+import concourse.mybir as mybir
+
+K, T, S, N, G, H, W, U = 512, 1024, 256, 512, 2048, 512, 128, 1024
+FLOPS = 2 * 2 * K * H * S + 2 * H * N * S
+
+F32 = mybir.dt.float32
+BF16 = mybir.dt.bfloat16
+I32 = mybir.dt.int32
+U32 = mybir.dt.uint32
+U16 = mybir.dt.uint16
+U8 = mybir.dt.uint8
+FP8X4 = mybir.dt.float8_e4m3fn_x4
+ALU = mybir.AluOpType
+COPY = mybir.ActivationFunctionType.Copy
+
+P = 128
+PACK = 4
+HALF = S // 2
+LIST_HALF = HALF // 16
+SPARE = 16
+
+
+def tile_picked_haqorddpags_none_p_kernel(
+    tc, x_words, x_scales, d_words, d_scales, gn, w1, offs, ka, kb, n1, n2, n3, n4, n5, out
+):
+    nc = tc.nc
+    with ExitStack() as ctx:
+        held = ctx.enter_context(tc.tile_pool(name="held", bufs=1))
+        psum = ctx.enter_context(tc.psum_pool(name="psum", bufs=1))
+
+        def load_list(src, name):
+            tile = held.tile(list(src.shape), U16, name=name)
+            nc.sync.dma_start(tile[:], src)
+            return tile
+
+        x_scale_table = held.tile([P, T], U8, name="x_scale_table")
+        d_scale_table = held.tile([P, G], U8, name="d_scale_table")
+
+        def load_scale_rows(table, rows):
+            words = rows.bitcast(I32)
+            nc.sync.dma_start(table[:].bitcast(I32), words.unsqueeze(1).broadcast_to([16, 8, words.shape[1]]))
+
+        offs_l = load_list(offs, "offs_l")
+        load_scale_rows(x_scale_table, x_scales[0])
+        ka_l = load_list(ka, "ka_l")
+        load_scale_rows(d_scale_table, d_scales[0])
+        kb_l = load_list(kb, "kb_l")
+
+        d_word_table = held.tile([P, G], I32, name="d_word_table", tag="big")
+        nc.sync.dma_start(d_word_table[:], d_words[0].rearrange("p c r -> p (c r)").bitcast(I32))
+        x_word_table = held.tile([P, T], I32, name="x_word_table")
+        nc.sync.dma_start(x_word_table[:], x_words[0].rearrange("p c r -> p (c r)").bitcast(I32))
+
+        n1_l = load_list(n1, "n1_l")
+        n2_l = load_list(n2, "n2_l")
+        gain = held.tile([P, PACK], F32, name="gain")
+        nc.sync.dma_start(gain[:], gn.rearrange("(p t) o -> p (t o)", t=PACK))
+        n3_l = load_list(n3, "n3_l")
+        n5_l = load_list(n5, "n5_l")
+        n4_l = load_list(n4, "n4_l")
+
+        placed = held.tile([P, S + 2 * H], U8, name="placed", align_bytes=64)
+        nc.vector.memset(placed[:].bitcast(I32), 0)
+
+        pages = [held.tile([P, U], F32, name="page%d" % m) for m in range(N // P)]
+        nc.vector.memset(pages[0][:], 0.0)
+        for m in range(1, N // P):
+            nc.scalar.activation(pages[m][:], pages[0][:], COPY)
+
+        picked_bytes = held.tile([P, S + 2 * H], U8, name="picked_bytes")
+        nc.vector.tensor_copy(picked_bytes[:, 0:S], x_scale_table[:].indirect(offs_l[:]))
+        nc.vector.tensor_copy(picked_bytes[:, S : S + H], d_scale_table[:].indirect(ka_l[:]))
+        nc.vector.tensor_copy(picked_bytes[:, S + H : S + 2 * H], d_scale_table[:].indirect(kb_l[:]))
+        for s in range(4):
+            queue = nc.sync if s % 2 == 0 else nc.scalar
+            queue.dma_start(placed[:].bitcast(I32)[s:P:32, :], picked_bytes[:].bitcast(I32)[8 * s : P : 32, :])
+
+        d_picked = held.tile([P, 2, H], U32, name="d_picked")
+        nc.vector.tensor_copy(d_picked[:, 0, :], d_word_table[:].bitcast(U32).indirect(ka_l[:]))
+        nc.vector.tensor_copy(d_picked[:, 1, :], d_word_table[:].bitcast(U32).indirect(kb_l[:]))
+        x_picked = held.tile([P, S], U32, name="x_picked", align_bytes=64)
+        nc.vector.tensor_copy(x_picked[:], x_word_table[:].bitcast(U32).indirect(offs_l[:]))
+
+        w_raw = held.tile([P, PACK, N], F32, name="w_raw", tag="big")
+        nc.sync.dma_start(w_raw[:], w1.rearrange("(p j) n -> p j n", j=PACK))
+
+        z_half = [held.tile([P, HALF, PACK], BF16, name="z%d" % c, align_bytes=64) for c in range(2)]
+        d_words_by_slot = d_picked[:].bitcast(I32).rearrange("p a (m t) -> p a t m", t=PACK)
+        d_bytes_by_slot = placed[:, S : S + 2 * H].rearrange("p (a m t) -> p a t m", a=2, t=PACK)
+        for t in range(PACK):
+            dealt_words = held.tile([P, 2, P], U32, name="dealt_words%d" % t, align_bytes=64)
+            dealt_bytes = held.tile([P, 2, P], U8, name="dealt_bytes%d" % t, align_bytes=64)
+            nc.vector.tensor_copy(dealt_words[:].bitcast(I32), d_words_by_slot[:, :, t, :])
+            nc.vector.tensor_copy(dealt_bytes[:], d_bytes_by_slot[:, :, t, :])
+            acc = psum.tile([P, S], F32, name="h_acc%d" % t, tag="bank%d" % t)
+            for a in range(2):
+                nc.tensor.matmul_mx(
+                    out=acc[:],
+                    lhsT=dealt_words[:, a, :].bitcast(FP8X4),
+                    lhsT_scale=dealt_bytes[:, a, :],
+                    rhs=x_picked[:].bitcast(FP8X4),
+                    rhs_scale=placed[:, 0:S],
+                    start=(a == 0),
+                    stop=(a == 1),
+                )
+            h = held.tile([P, S], F32, name="h%d" % t)
+            nc.vector.tensor_scalar(h[:], acc[:], 0.0625, None, ALU.mult)
+            pa = held.tile([P, W], F32, name="pa%d" % t)
+            pb = held.tile([P, W], F32, name="pb%d" % t)
+            nc.scalar.activation(pa[:], h[:].indirect(n1_l[:]), COPY)
+            nc.scalar.activation(pb[:], h[:].indirect(n2_l[:]), COPY)
+            ra = held.tile([P, W], F32, name="ra%d" % t)
+            rb = held.tile([P, W], F32, name="rb%d" % t)
+            nc.vector.tensor_tensor(ra[:], pa[:], pb[:], ALU.max)
+            nc.vector.tensor_tensor(rb[:], pa[:], pb[:], ALU.min)
+            dt = held.tile([P, S + SPARE], F32, name="dt%d" % t)
+            nc.scalar.activation(dt[:].indirect(n1_l[:]), ra[:], COPY)
+            nc.scalar.activation(dt[:].indirect(n2_l[:]), rb[:], COPY)
+            if t < PACK - 1:
+                other = held.tile([P, S], F32, name="other%d" % t)
+                nc.scalar.activation(other[:], dt[:].indirect(n3_l[:]), COPY)
+                diff = held.tile([P, S], F32, name="diff%d" % t)
+                nc.vector.tensor_tensor(diff[:], dt[:, 0:S], other[:], ALU.subtract)
+                for c in range(2):
+                    nc.vector.tensor_scalar(
+                        z_half[c][:, :, t], diff[:, c * HALF : (c + 1) * HALF], gain[:, t : t + 1], None, ALU.mult
+                    )
+                continue
+            for c in range(2):
+                other = held.tile([P, HALF], F32, name="other%d_%d" % (t, c))
+                nc.scalar.activation(
+                    other[:],
+                    dt[:].indirect(n3_l[:, c * LIST_HALF : (c + 1) * LIST_HALF]),
+                    COPY,
+                    scale=gain[:, t : t + 1],
+                )
+                nc.vector.scalar_tensor_tensor(
+                    z_half[c][:, :, t],
+                    dt[:, c * HALF : (c + 1) * HALF],
+                    gain[:, t : t + 1],
+                    other[:],
+                    ALU.mult,
+                    ALU.subtract,
+                )
+
+        w_codes = held.tile([P, N], U32, name="w_codes", align_bytes=64)
+        w_scales = held.tile([P, N], U8, name="w_scales", align_bytes=64)
+        for m in range(N // P):
+            cols = slice(m * P, (m + 1) * P)
+            w_grouped = held.tile([P, P, PACK], BF16, name="w_grouped%d" % m, align_bytes=64)
+            nc.vector.tensor_copy(w_grouped[:], w_raw[:, :, cols].rearrange("p j n -> p n j"))
+            nc.vector.quantize_mx(
+                out=w_codes[:, cols].bitcast(FP8X4),
+                scales=w_scales[:, cols],
+                in_=w_grouped[:].rearrange("p n j -> p (n j)"),
+            )
+
+        z_codes = held.tile([P, S], U32, name="z_codes", align_bytes=64)
+        z_scales = held.tile([P, S], U8, name="z_scales", align_bytes=64)
+        for c in range(2):
+            cols = slice(c * HALF, (c + 1) * HALF)
+            nc.vector.quantize_mx(
+                out=z_codes[:, cols].bitcast(FP8X4),
+                scales=z_scales[:, cols],
+                in_=z_half[c][:].rearrange("p n j -> p (n j)"),
+            )
+
+        def second_product(acc, m, cols):
+            nc.tensor.matmul_mx(
+                out=acc[:],
+                lhsT=w_codes[:, m * P : (m + 1) * P].bitcast(FP8X4),
+                lhsT_scale=w_scales[:, m * P : (m + 1) * P],
+                rhs=z_codes[:, cols].bitcast(FP8X4),
+                rhs_scale=z_scales[:, cols],
+                start=True,
+                stop=True,
+            )
+
+        for m in range(N // P):
+            h2 = held.tile([P, S + SPARE], F32, name="h2_%d" % m)
+            if m == 0:
+                for c in range(2):
+                    cols = slice(c * HALF, (c + 1) * HALF)
+                    acc = psum.tile([P, HALF], F32, name="h2_acc0_%d" % c, tag="bank%d" % (4 + c))
+                    second_product(acc, m, cols)
+                    nc.scalar.copy(h2[:, cols], acc[:])
+            else:
+                acc = psum.tile([P, S], F32, name="h2_acc%d" % m, tag="bank%d" % ((5 + m) % 8))
+                second_product(acc, m, slice(0, S))
+                nc.vector.tensor_copy(h2[:, 0:S], acc[:])
+            partner = held.tile([P, S], F32, name="partner%d" % m)
+            nc.scalar.activation(partner[:], h2[:].indirect(n5_l[:]), COPY)
+            nw = held.tile([P, S], F32, name="nw%d" % m)
+            nc.vector.tensor_tensor(nw[:], h2[:, 0:S], partner[:], ALU.max)
+            nc.scalar.activation(pages[m][:].indirect(n4_l[:]), nw[:], COPY)
+            nc.sync.dma_start(out[m * P : (m + 1) * P, :], pages[m][:])

@@ -36,27 +36,27 @@ def tile_picked_haqorddpags_none_p_kernel(
             return tile
 
         x_scale_table = held.tile([P, T], U8, name="x_scale_table")
-        d_scale_table = held.tile([P, G], U8, name="d_scale_table")
+        d_scale_table = held.tile([P, G], U8, name="d_scale_table", tag="big")
 
         def load_scale_rows(table, rows):
-            words = rows.bitcast(I32)
-            nc.sync.dma_start(table[:].bitcast(I32), words.unsqueeze(1).broadcast_to([16, 8, words.shape[1]]))
+            nc.sync.dma_start(table[:].bitcast(I32)[0:P:8, :], rows.bitcast(I32))
 
+        nc.vector.memset(x_scale_table[:].bitcast(I32), 0)
+        nc.vector.memset(d_scale_table[:].bitcast(I32), 0)
         offs_l = load_list(offs, "offs_l")
-        load_scale_rows(x_scale_table, x_scales[0])
         ka_l = load_list(ka, "ka_l")
-        load_scale_rows(d_scale_table, d_scales[0])
         kb_l = load_list(kb, "kb_l")
-
-        d_word_table = held.tile([P, G], I32, name="d_word_table", tag="big")
-        nc.sync.dma_start(d_word_table[:], d_words[0].rearrange("p c r -> p (c r)").bitcast(I32))
-        x_word_table = held.tile([P, T], I32, name="x_word_table")
-        nc.sync.dma_start(x_word_table[:], x_words[0].rearrange("p c r -> p (c r)").bitcast(I32))
-
+        load_scale_rows(x_scale_table, x_scales[0])
+        load_scale_rows(d_scale_table, d_scales[0])
         n1_l = load_list(n1, "n1_l")
         n2_l = load_list(n2, "n2_l")
+
+        d_word_table = held.tile([P, G], I32, name="d_word_table")
+        nc.sync.dma_start(d_word_table[:], d_words[0].rearrange("p c r -> p (c r)").bitcast(I32))
         gain = held.tile([P, PACK], F32, name="gain")
         nc.sync.dma_start(gain[:], gn.rearrange("(p t) o -> p (t o)", t=PACK))
+        x_word_table = held.tile([P, T], I32, name="x_word_table")
+        nc.sync.dma_start(x_word_table[:], x_words[0].rearrange("p c r -> p (c r)").bitcast(I32))
         n3_l = load_list(n3, "n3_l")
         n5_l = load_list(n5, "n5_l")
         n4_l = load_list(n4, "n4_l")
@@ -69,7 +69,7 @@ def tile_picked_haqorddpags_none_p_kernel(
         for m in range(1, N // P):
             nc.scalar.activation(pages[m][:], pages[0][:], COPY)
 
-        picked_bytes = held.tile([P, S + 2 * H], U8, name="picked_bytes")
+        picked_bytes = held.tile([P, S + 2 * H], U8, name="picked_bytes", tag="picked", align_bytes=64)
         nc.vector.tensor_copy(picked_bytes[:, 0:S], x_scale_table[:].indirect(offs_l[:]))
         nc.vector.tensor_copy(picked_bytes[:, S : S + H], d_scale_table[:].indirect(ka_l[:]))
         nc.vector.tensor_copy(picked_bytes[:, S + H : S + 2 * H], d_scale_table[:].indirect(kb_l[:]))
@@ -77,23 +77,26 @@ def tile_picked_haqorddpags_none_p_kernel(
             queue = nc.sync if s % 2 == 0 else nc.scalar
             queue.dma_start(placed[:].bitcast(I32)[s:P:32, :], picked_bytes[:].bitcast(I32)[8 * s : P : 32, :])
 
-        d_picked = held.tile([P, 2, H], U32, name="d_picked")
-        nc.vector.tensor_copy(d_picked[:, 0, :], d_word_table[:].bitcast(U32).indirect(ka_l[:]))
-        nc.vector.tensor_copy(d_picked[:, 1, :], d_word_table[:].bitcast(U32).indirect(kb_l[:]))
+        d_picked = [held.tile([P, H], U32, name="d_picked%d" % a) for a in range(2)]
+        nc.vector.tensor_copy(d_picked[0][:], d_word_table[:].bitcast(U32).indirect(ka_l[:]))
+        first_words = held.tile([P, 2, P], U32, name="dealt_words0", align_bytes=64)
+        nc.vector.tensor_copy(first_words[:, 0, :].bitcast(I32), d_picked[0][:].bitcast(I32)[:, 0:H:PACK])
         x_picked = held.tile([P, S], U32, name="x_picked", align_bytes=64)
         nc.vector.tensor_copy(x_picked[:], x_word_table[:].bitcast(U32).indirect(offs_l[:]))
+        nc.vector.tensor_copy(d_picked[1][:], d_word_table[:].bitcast(U32).indirect(kb_l[:]))
 
         w_raw = held.tile([P, PACK, N], F32, name="w_raw", tag="big")
         nc.sync.dma_start(w_raw[:], w1.rearrange("(p j) n -> p j n", j=PACK))
 
         z_half = [held.tile([P, HALF, PACK], BF16, name="z%d" % c, align_bytes=64) for c in range(2)]
-        d_words_by_slot = d_picked[:].bitcast(I32).rearrange("p a (m t) -> p a t m", t=PACK)
         d_bytes_by_slot = placed[:, S : S + 2 * H].rearrange("p (a m t) -> p a t m", a=2, t=PACK)
+        later_words = held.tile([P, PACK - 1, 2, P], U32, name="later_words", tag="picked", align_bytes=64)
         for t in range(PACK):
-            dealt_words = held.tile([P, 2, P], U32, name="dealt_words%d" % t, align_bytes=64)
+            dealt_words = first_words[:] if t == 0 else later_words[:, t - 1, :, :]
             dealt_bytes = held.tile([P, 2, P], U8, name="dealt_bytes%d" % t, align_bytes=64)
-            nc.vector.tensor_copy(dealt_words[:].bitcast(I32), d_words_by_slot[:, :, t, :])
             nc.vector.tensor_copy(dealt_bytes[:], d_bytes_by_slot[:, :, t, :])
+            for a in range(1 if t == 0 else 0, 2):
+                nc.vector.tensor_copy(dealt_words[:, a, :].bitcast(I32), d_picked[a][:].bitcast(I32)[:, t:H:PACK])
             acc = psum.tile([P, S], F32, name="h_acc%d" % t, tag="bank%d" % t)
             for a in range(2):
                 nc.tensor.matmul_mx(
@@ -106,13 +109,16 @@ def tile_picked_haqorddpags_none_p_kernel(
                     stop=(a == 1),
                 )
             h = held.tile([P, S], F32, name="h%d" % t)
-            nc.vector.tensor_scalar(h[:], acc[:], 0.0625, None, ALU.mult)
+            if t == 0:
+                nc.scalar.activation(h[:], acc[:], COPY, scale=0.0625)
+            else:
+                nc.vector.tensor_scalar(h[:], acc[:], 0.0625, None, ALU.mult)
             pa = held.tile([P, W], F32, name="pa%d" % t)
             pb = held.tile([P, W], F32, name="pb%d" % t)
             nc.scalar.activation(pa[:], h[:].indirect(n1_l[:]), COPY)
             nc.scalar.activation(pb[:], h[:].indirect(n2_l[:]), COPY)
             ra = held.tile([P, W], F32, name="ra%d" % t)
-            rb = held.tile([P, W], F32, name="rb%d" % t)
+            rb = held.tile([P, W], F32, name="rb%d" % t, tag="rb%d" % min(t, PACK - 2))
             nc.vector.tensor_tensor(ra[:], pa[:], pb[:], ALU.max)
             nc.vector.tensor_tensor(rb[:], pa[:], pb[:], ALU.min)
             dt = held.tile([P, S + SPARE], F32, name="dt%d" % t)

from contextlib import ExitStack

import concourse.mybir as mybir

K, T, S, N, G, H, W, U = 512, 1024, 256, 512, 2048, 512, 128, 1024
FLOPS = 2 * 2 * K * H * S + 2 * H * N * S

F32 = mybir.dt.float32
BF16 = mybir.dt.bfloat16
I32 = mybir.dt.int32
U32 = mybir.dt.uint32
U16 = mybir.dt.uint16
U8 = mybir.dt.uint8
FP8X4 = mybir.dt.float8_e4m3fn_x4
ALU = mybir.AluOpType
COPY = mybir.ActivationFunctionType.Copy

P = 128
PACK = 4
HALF = S // 2
LIST_HALF = HALF // 16
SPARE = 16


def tile_picked_haqorddpags_none_p_kernel(
    tc, x_words, x_scales, d_words, d_scales, gn, w1, offs, ka, kb, n1, n2, n3, n4, n5, out
):
    nc = tc.nc
    with ExitStack() as ctx:
        held = ctx.enter_context(tc.tile_pool(name="held", bufs=1))
        psum = ctx.enter_context(tc.psum_pool(name="psum", bufs=1))

        def load_list(src, name):
            tile = held.tile(list(src.shape), U16, name=name)
            nc.sync.dma_start(tile[:], src)
            return tile

        x_scale_table = held.tile([P, T], U8, name="x_scale_table")
        d_scale_table = held.tile([P, G], U8, name="d_scale_table", tag="big")

        def load_scale_rows(table, rows):
            nc.sync.dma_start(table[:].bitcast(I32)[0:P:8, :], rows.bitcast(I32))

        nc.vector.memset(x_scale_table[:].bitcast(I32), 0)
        nc.vector.memset(d_scale_table[:].bitcast(I32), 0)
        offs_l = load_list(offs, "offs_l")
        ka_l = load_list(ka, "ka_l")
        kb_l = load_list(kb, "kb_l")
        load_scale_rows(x_scale_table, x_scales[0])
        load_scale_rows(d_scale_table, d_scales[0])
        n1_l = load_list(n1, "n1_l")
        n2_l = load_list(n2, "n2_l")

        d_word_table = held.tile([P, G], I32, name="d_word_table")
        nc.sync.dma_start(d_word_table[:], d_words[0].rearrange("p c r -> p (c r)").bitcast(I32))
        gain = held.tile([P, PACK], F32, name="gain")
        nc.sync.dma_start(gain[:], gn.rearrange("(p t) o -> p (t o)", t=PACK))
        x_word_table = held.tile([P, T], I32, name="x_word_table")
        nc.sync.dma_start(x_word_table[:], x_words[0].rearrange("p c r -> p (c r)").bitcast(I32))
        n3_l = load_list(n3, "n3_l")
        n5_l = load_list(n5, "n5_l")
        n4_l = load_list(n4, "n4_l")

        placed = held.tile([P, S + 2 * H], U8, name="placed", align_bytes=64)
        nc.vector.memset(placed[:].bitcast(I32), 0)

        pages = [held.tile([P, U], F32, name="page%d" % m) for m in range(N // P)]
        nc.vector.memset(pages[0][:], 0.0)
        for m in range(1, N // P):
            nc.scalar.activation(pages[m][:], pages[0][:], COPY)

        picked_bytes = held.tile([P, S + 2 * H], U8, name="picked_bytes", tag="picked", align_bytes=64)
        nc.vector.tensor_copy(picked_bytes[:, 0:S], x_scale_table[:].indirect(offs_l[:]))
        nc.vector.tensor_copy(picked_bytes[:, S : S + H], d_scale_table[:].indirect(ka_l[:]))
        nc.vector.tensor_copy(picked_bytes[:, S + H : S + 2 * H], d_scale_table[:].indirect(kb_l[:]))
        for s in range(4):
            queue = nc.sync if s % 2 == 0 else nc.scalar
            queue.dma_start(placed[:].bitcast(I32)[s:P:32, :], picked_bytes[:].bitcast(I32)[8 * s : P : 32, :])

        d_picked = [held.tile([P, H], U32, name="d_picked%d" % a) for a in range(2)]
        nc.vector.tensor_copy(d_picked[0][:], d_word_table[:].bitcast(U32).indirect(ka_l[:]))
        first_words = held.tile([P, 2, P], U32, name="dealt_words0", align_bytes=64)
        nc.vector.tensor_copy(first_words[:, 0, :].bitcast(I32), d_picked[0][:].bitcast(I32)[:, 0:H:PACK])
        x_picked = held.tile([P, S], U32, name="x_picked", align_bytes=64)
        nc.vector.tensor_copy(x_picked[:], x_word_table[:].bitcast(U32).indirect(offs_l[:]))
        nc.vector.tensor_copy(d_picked[1][:], d_word_table[:].bitcast(U32).indirect(kb_l[:]))

        w_raw = held.tile([P, PACK, N], F32, name="w_raw", tag="big")
        nc.sync.dma_start(w_raw[:], w1.rearrange("(p j) n -> p j n", j=PACK))

        z_half = [held.tile([P, HALF, PACK], BF16, name="z%d" % c, align_bytes=64) for c in range(2)]
        d_bytes_by_slot = placed[:, S : S + 2 * H].rearrange("p (a m t) -> p a t m", a=2, t=PACK)
        later_words = held.tile([P, PACK - 1, 2, P], U32, name="later_words", tag="picked", align_bytes=64)
        for t in range(PACK):
            dealt_words = first_words[:] if t == 0 else later_words[:, t - 1, :, :]
            dealt_bytes = held.tile([P, 2, P], U8, name="dealt_bytes%d" % t, align_bytes=64)
            nc.vector.tensor_copy(dealt_bytes[:], d_bytes_by_slot[:, :, t, :])
            for a in range(1 if t == 0 else 0, 2):
                nc.vector.tensor_copy(dealt_words[:, a, :].bitcast(I32), d_picked[a][:].bitcast(I32)[:, t:H:PACK])
            acc = psum.tile([P, S], F32, name="h_acc%d" % t, tag="bank%d" % t)
            for a in range(2):
                nc.tensor.matmul_mx(
                    out=acc[:],
                    lhsT=dealt_words[:, a, :].bitcast(FP8X4),
                    lhsT_scale=dealt_bytes[:, a, :],
                    rhs=x_picked[:].bitcast(FP8X4),
                    rhs_scale=placed[:, 0:S],
                    start=(a == 0),
                    stop=(a == 1),
                )
            h = held.tile([P, S], F32, name="h%d" % t)
            if t == 0:
                nc.scalar.activation(h[:], acc[:], COPY, scale=0.0625)
            else:
                nc.vector.tensor_scalar(h[:], acc[:], 0.0625, None, ALU.mult)
            pa = held.tile([P, W], F32, name="pa%d" % t)
            pb = held.tile([P, W], F32, name="pb%d" % t)
            nc.scalar.activation(pa[:], h[:].indirect(n1_l[:]), COPY)
            nc.scalar.activation(pb[:], h[:].indirect(n2_l[:]), COPY)
            ra = held.tile([P, W], F32, name="ra%d" % t)
            rb = held.tile([P, W], F32, name="rb%d" % t, tag="rb%d" % min(t, PACK - 2))
            nc.vector.tensor_tensor(ra[:], pa[:], pb[:], ALU.max)
            nc.vector.tensor_tensor(rb[:], pa[:], pb[:], ALU.min)
            dt = held.tile([P, S + SPARE], F32, name="dt%d" % t)
            nc.scalar.activation(dt[:].indirect(n1_l[:]), ra[:], COPY)
            nc.scalar.activation(dt[:].indirect(n2_l[:]), rb[:], COPY)
            if t < PACK - 1:
                other = held.tile([P, S], F32, name="other%d" % t)
                nc.scalar.activation(other[:], dt[:].indirect(n3_l[:]), COPY)
                diff = held.tile([P, S], F32, name="diff%d" % t)
                nc.vector.tensor_tensor(diff[:], dt[:, 0:S], other[:], ALU.subtract)
                for c in range(2):
                    nc.vector.tensor_scalar(
                        z_half[c][:, :, t], diff[:, c * HALF : (c + 1) * HALF], gain[:, t : t + 1], None, ALU.mult
                    )
                continue
            for c in range(2):
                other = held.tile([P, HALF], F32, name="other%d_%d" % (t, c))
                nc.scalar.activation(
                    other[:],
                    dt[:].indirect(n3_l[:, c * LIST_HALF : (c + 1) * LIST_HALF]),
                    COPY,
                    scale=gain[:, t : t + 1],
                )
                nc.vector.scalar_tensor_tensor(
                    z_half[c][:, :, t],
                    dt[:, c * HALF : (c + 1) * HALF],
                    gain[:, t : t + 1],
                    other[:],
                    ALU.mult,
                    ALU.subtract,
                )

        w_codes = held.tile([P, N], U32, name="w_codes", align_bytes=64)
        w_scales = held.tile([P, N], U8, name="w_scales", align_bytes=64)
        for m in range(N // P):
            cols = slice(m * P, (m + 1) * P)
            w_grouped = held.tile([P, P, PACK], BF16, name="w_grouped%d" % m, align_bytes=64)
            nc.vector.tensor_copy(w_grouped[:], w_raw[:, :, cols].rearrange("p j n -> p n j"))
            nc.vector.quantize_mx(
                out=w_codes[:, cols].bitcast(FP8X4),
                scales=w_scales[:, cols],
                in_=w_grouped[:].rearrange("p n j -> p (n j)"),
            )

        z_codes = held.tile([P, S], U32, name="z_codes", align_bytes=64)
        z_scales = held.tile([P, S], U8, name="z_scales", align_bytes=64)
        for c in range(2):
            cols = slice(c * HALF, (c + 1) * HALF)
            nc.vector.quantize_mx(
                out=z_codes[:, cols].bitcast(FP8X4),
                scales=z_scales[:, cols],
                in_=z_half[c][:].rearrange("p n j -> p (n j)"),
            )

        def second_product(acc, m, cols):
            nc.tensor.matmul_mx(
                out=acc[:],
                lhsT=w_codes[:, m * P : (m + 1) * P].bitcast(FP8X4),
                lhsT_scale=w_scales[:, m * P : (m + 1) * P],
                rhs=z_codes[:, cols].bitcast(FP8X4),
                rhs_scale=z_scales[:, cols],
                start=True,
                stop=True,
            )

        for m in range(N // P):
            h2 = held.tile([P, S + SPARE], F32, name="h2_%d" % m)
            if m == 0:
                for c in range(2):
                    cols = slice(c * HALF, (c + 1) * HALF)
                    acc = psum.tile([P, HALF], F32, name="h2_acc0_%d" % c, tag="bank%d" % (4 + c))
                    second_product(acc, m, cols)
                    nc.scalar.copy(h2[:, cols], acc[:])
            else:
                acc = psum.tile([P, S], F32, name="h2_acc%d" % m, tag="bank%d" % ((5 + m) % 8))
                second_product(acc, m, slice(0, S))
                nc.vector.tensor_copy(h2[:, 0:S], acc[:])
            partner = held.tile([P, S], F32, name="partner%d" % m)
            nc.scalar.activation(partner[:], h2[:].indirect(n5_l[:]), COPY)
            nw = held.tile([P, S], F32, name="nw%d" % m)
            nc.vector.tensor_tensor(nw[:], h2[:, 0:S], partner[:], ALU.max)
            nc.scalar.activation(pages[m][:].indirect(n4_l[:]), nw[:], COPY)
            nc.sync.dma_start(out[m * P : (m + 1) * P, :], pages[m][:])
